import numpy as np
import ml_dtypes


def mxq(x, axis, fmt="e4m3"):
    dtype, down = {"e4m3": (ml_dtypes.float8_e4m3fn, 7), "e5m2": (ml_dtypes.float8_e5m2, 14)}[fmt]
    v = np.moveaxis(np.asarray(x, np.float32).astype(ml_dtypes.bfloat16).astype(np.float64), axis, -1)
    blocks = v.reshape(v.shape[:-1] + (-1, 32))
    amax = np.abs(blocks).max(-1, keepdims=True)
    byte = np.maximum(np.where(amax > 0, np.frexp(amax)[1] - 1 + 127, 0) - down, 1)
    scale = np.exp2(byte - 127.0)
    codes = (blocks / scale).astype(np.float32).astype(dtype).astype(np.float64)
    return np.moveaxis((codes * scale).reshape(v.shape), -1, axis)


WIDE = False


def mx_kscale(k):
    if not WIDE:
        return np.ones(k)
    levels = np.array([10, -10, 5, -5, 0])
    if k % 512:
        return np.exp2(np.random.permutation(np.resize(levels, k // 32))).repeat(32)
    a = np.empty((k // 512, 16))
    for p in range(k // 512):
        a[p, :8] = np.random.permutation(np.resize(levels, 8))
        for g in range(8):
            far = levels[np.abs(levels - a[p, g]) >= 10]
            a[p, g + 8] = far[np.random.randint(len(far))]
    return np.exp2(a.ravel()).repeat(32)


def f64(x):
    return np.asarray(x).astype(np.float64)


def striped(idx):
    return np.tile(idx.reshape(-1, 16).T, (8, 1)).astype(np.uint16)


def unstriped(offs):
    return offs[:16].T.reshape(-1).astype(np.int64)


def relu(v):
    return np.maximum(v, 0.0)

def planes(y):
    n, m = y.shape
    v = y.astype(np.float32).astype(ml_dtypes.bfloat16).astype(np.float64).reshape(n // 32, 32, m)
    top = np.abs(v).max(1)
    byte = np.clip(np.where(top > 0, np.frexp(top)[1] - 1 + 127 - 7, 1), 1, 254)
    codes = (v * np.exp2(127.0 - byte)[:, None, :]).reshape(n, m).astype(np.float32).astype(ml_dtypes.float8_e4m3fn).view(np.uint8)
    words = codes.reshape(n // 512, 128, 4, m).transpose(0, 1, 3, 2)
    return np.ascontiguousarray(words), np.ascontiguousarray(byte.astype(np.uint8).reshape(n // 512, 16, m))


K, T, S, V, H = 512, 1024, 512, 256, 512


def setup_inputs():
    n = np.random.standard_normal
    s = mx_kscale(K)[:, None]
    u = mx_kscale(H)
    return {
        "xT": (n((K, T)) * s).astype(np.float32),
        "w1": (n((K, H)) / np.sqrt(K) / s * u).astype(np.float32),
        "w2": (n((H, H)) / np.sqrt(H) / u[:, None]).astype(np.float32),
        "offs": striped(np.random.permutation(T)[:S]),
    }


def reference(xT, w1, w2, offs):
    xq = mxq(f64(xT)[:, unstriped(offs)], 0, "e4m3")
    h = relu(mxq(f64(w1), 0, "e4m3").T @ xq)
    z = np.abs(h[:, :V] - h[:, V:2 * V])
    out_0 = mxq(f64(w2), 0, "e4m3").T @ mxq(z, 0, "e4m3")
    return (out_0,) + planes(out_0)

@@ -1,0 +1,174 @@
+from contextlib import ExitStack
+
+import concourse.mybir as mybir
+
+K, T, S, V, H = 512, 1024, 512, 256, 512
+FLOPS = 2 * K * H * S + 2 * H * H * V
+
+F32 = mybir.dt.float32
+BF16 = mybir.dt.bfloat16
+I32 = mybir.dt.int32
+U32 = mybir.dt.uint32
+U16 = mybir.dt.uint16
+U8 = mybir.dt.uint8
+FP8X4 = mybir.dt.float8_e4m3fn_x4
+ACT = mybir.ActivationFunctionType
+ALU = mybir.AluOpType
+
+P = 128
+PACK = 4
+CH = 128
+
+
+def tile_picked_siam_abs_lo_kernel(tc, xT, w1, w2, offs, out_0, out_1, out_2):
+    nc = tc.nc
+    with ExitStack() as ctx:
+        keep = ctx.enter_context(tc.tile_pool(name="keep", bufs=1))
+        psum = ctx.enter_context(tc.psum_pool(name="psum", bufs=1))
+
+        def sb(shape, dtype, name):
+            return keep.tile(shape, dtype, name=name, align_bytes=64)
+
+        def quant(words, scales, src):
+            nc.vector.quantize_mx(out=words.bitcast(FP8X4), scales=scales, in_=src)
+
+        offsets = keep.tile([P, S // 16], U16, name="offsets")
+        nc.sync.dma_start(offsets[:], offs)
+        x_rows = xT.rearrange("(p j) c -> p j c", j=PACK)
+        planes = []
+        for j in range(PACK):
+            plane = sb([P, T], F32, f"plane{j}")
+            nc.sync.dma_start(plane[:], x_rows[:, j, :])
+            planes.append(plane)
+        w1_raw = sb([P, PACK, H], F32, "w1_raw")
+        nc.sync.dma_start(w1_raw[:], w1.rearrange("(p j) c -> p j c", j=PACK))
+        w2_rows = w2.rearrange("(p j) c -> p j c", j=PACK)
+        w2_raw = []
+        for u in range(2):
+            half = sb([P, PACK, H // 2], F32, f"w2_raw{u}")
+            nc.sync.dma_start(half[:], w2_rows[:, :, u * 256 : (u + 1) * 256])
+            w2_raw.append(half)
+
+        warm = sb([P, 8], F32, "warm")
+        warm2 = sb([P, 8], F32, "warm2")
+        nc.gpsimd.memset(warm[:], 0.0)
+        nc.scalar.activation(warm2[:], warm[:], ACT.Relu)
+
+        g01 = sb([P, 2, S], F32, "g01")
+        g23 = [sb([P, 2, V], F32, f"g23_{h}") for h in range(2)]
+        xg = [sb([P, V, PACK], BF16, f"xg{h}") for h in range(2)]
+        xw = [sb([P, V], U32, f"xw{h}") for h in range(2)]
+        xs = [sb([P, V], U8, f"xs{h}") for h in range(2)]
+
+        def weave_views(h, pair, src):
+            dst = xg[h][:, :, 2 * pair : 2 * pair + 2].rearrange("p (c i) t -> p c t i", i=4)
+            return dst, src.rearrange("p t (c i) -> p c t i", i=4)
+
+        for j in range(2):
+            nc.vector.tensor_copy(g01[:, j, :], planes[j][:].indirect(offsets[:]))
+        for h in (1, 0):
+            dst, src = weave_views(h, 0, g01[:, :, h * V : (h + 1) * V])
+            nc.scalar.activation(dst, src, ACT.Copy)
+        for j in range(2):
+            for h in (1, 0):
+                nc.vector.tensor_copy(g23[h][:, j, :], planes[2 + j][:].indirect(offsets[:, h * 16 : (h + 1) * 16]))
+        dst, src = weave_views(1, 1, g23[1][:])
+        nc.scalar.activation(dst, src, ACT.Copy)
+        dst, src = weave_views(0, 1, g23[0][:])
+        nc.vector.tensor_copy(dst, src)
+        for h in (1, 0):
+            quant(xw[h][:], xs[h][:], xg[h][:].rearrange("p c t -> p (c t)"))
+
+        w1_view = w1_raw[:].rearrange("p j (m t) -> p m j t", t=PACK)
+        w1g = [sb([P, 2, P, PACK], BF16, f"w1g{u}") for u in range(2)]
+        w1w = sb([P, H], U32, "w1w")
+        w1s = sb([P, H], U8, "w1s")
+        nc.vector.tensor_copy(w1g[0][:].rearrange("p t m j -> p m j t"), w1_view[:, :, :, 0:2])
+        nc.scalar.activation(w1g[1][:].rearrange("p t m j -> p m j t"), w1_view[:, :, :, 2:4], ACT.Copy)
+        for t in range(PACK):
+            cols = slice(t * P, (t + 1) * P)
+            quant(w1w[:, cols], w1s[:, cols], w1g[t // 2][:, t % 2, :, :].rearrange("p m j -> p (m j)"))
+
+        hp = [[psum.tile([P, PACK, CH], F32, name=f"hp{h}{c}") for c in range(2)] for h in range(2)]
+
+        def mm(out, lw, ls, t, rw, rs):
+            cols = slice(t * P, (t + 1) * P)
+            nc.tensor.matmul_mx(out=out, lhsT=lw[:, cols].bitcast(FP8X4), lhsT_scale=ls[:, cols],
+                                rhs=rw.bitcast(FP8X4), rhs_scale=rs, start=True, stop=True)
+
+        def mm1(h, c, t):
+            cc = slice(c * CH, (c + 1) * CH)
+            mm(hp[h][c][:, t, :], w1w, w1s, t, xw[h][:, cc], xs[h][:, cc])
+
+        for t in range(PACK):
+            for h in (1, 0):
+                mm1(h, 0, t)
+        for h in (1, 0):
+            for t in range(PACK):
+                mm1(h, 1, t)
+
+        w2g = [sb([P, PACK, P // 2, PACK], BF16, f"w2g{u}") for u in range(2)]
+        w2w = sb([P, H], U32, "w2w")
+        w2s = sb([P, H], U8, "w2s")
+
+        def w2_views(u):
+            return w2g[u][:].rearrange("p t m j -> p m j t"), w2_raw[u][:].rearrange("p j (m t) -> p m j t", t=PACK)
+
+        def w2_quant(u):
+            for t in range(PACK):
+                cols = slice(t * P + u * 64, t * P + (u + 1) * 64)
+                quant(w2w[:, cols], w2s[:, cols], w2g[u][:, t, :, :].rearrange("p m j -> p (m j)"))
+
+        rb = [sb([P, CH, PACK], F32, f"rb{c}") for c in range(2)]
+        dz = [sb([P, CH, PACK], F32, f"dz{c}") for c in range(2)]
+        zb = [sb([P, CH * PACK], BF16, f"zb{c}") for c in range(2)]
+        zw = [sb([P, CH], U32, f"zw{c}") for c in range(2)]
+        zs = [sb([P, CH], U8, f"zs{c}") for c in range(2)]
+
+        def relu_b(c):
+            nc.scalar.activation(rb[c][:], hp[1][c][:].rearrange("p t v -> p v t"), ACT.Relu)
+
+        def diff(c):
+            nc.vector.scalar_tensor_tensor(dz[c][:], hp[0][c][:].rearrange("p t v -> p v t"), 0.0, rb[c][:],
+                                           ALU.max, ALU.subtract)
+
+        def mag(c):
+            nc.scalar.activation(zb[c][:], dz[c][:].rearrange("p v t -> p (v t)"), ACT.Abs)
+
+        dst, src = w2_views(0)
+        nc.vector.tensor_copy(dst, src)
+        relu_b(0)
+        w2_quant(0)
+        diff(0)
+        relu_b(1)
+        dst, src = w2_views(1)
+        nc.vector.tensor_copy(dst, src)
+        mag(0)
+        diff(1)
+        w2_quant(1)
+        quant(zw[0][:], zs[0][:], zb[0][:])
+        mag(1)
+        quant(zw[1][:], zs[1][:], zb[1][:])
+
+        yp = [[psum.tile([P, 2, CH], F32, name=f"yp{c}{u}") for u in range(2)] for c in range(2)]
+        yf = [sb([P, PACK, CH], F32, f"yf{c}") for c in range(2)]
+        yb = [sb([P, CH, PACK], BF16, f"yb{c}") for c in range(2)]
+        yw = sb([P, V], U32, "yw")
+        ys = sb([P, V], U8, "ys")
+        y_rows = out_0.rearrange("(p t) v -> p t v", t=PACK)
+        y_words = out_1[0].rearrange("p c r -> p (c r)").bitcast(I32)
+        y_scales = out_2[0].bitcast(I32)
+        for c in range(2):
+            cc = slice(c * CH, (c + 1) * CH)
+            for t in range(PACK):
+                mm(yp[c][t // 2][:, t % 2, :], w2w, w2s, t, zw[c][:], zs[c][:])
+            for u in range(2):
+                nc.scalar.copy(yf[c][:, 2 * u : 2 * u + 2, :], yp[c][u][:])
+            nc.sync.dma_start(y_rows[:, :, cc], yf[c][:])
+            nc.vector.tensor_copy(yb[c][:].rearrange("p (c i) t -> p c t i", i=4),
+                                  yf[c][:].rearrange("p t (c i) -> p c t i", i=4))
+            quant(yw[:, cc], ys[:, cc], yb[c][:].rearrange("p c t -> p (c t)"))
+            nc.sync.dma_start(y_words[:, cc], yw[:, cc].bitcast(I32))
+        for q in range(4):
+            eng = nc.sync if q % 2 == 0 else nc.scalar
+            eng.dma_start(y_scales[4 * q : 4 * q + 4, :], ys[32 * q : 32 * q + 4, :].bitcast(I32))

@@ -26,8 +26,8 @@ def tile_picked_siam_abs_lo_kernel(tc, xT, w1, w2, offs, out_0, out_1, out_2):
         keep = ctx.enter_context(tc.tile_pool(name="keep", bufs=1))
         psum = ctx.enter_context(tc.psum_pool(name="psum", bufs=1))
 
-        def sb(shape, dtype, name):
-            return keep.tile(shape, dtype, name=name, align_bytes=64)
+        def sb(shape, dtype, name, tag=None):
+            return keep.tile(shape, dtype, name=name, tag=tag or name, align_bytes=64)
 
         def quant(words, scales, src):
             nc.vector.quantize_mx(out=words.bitcast(FP8X4), scales=scales, in_=src)
@@ -40,84 +40,81 @@ def tile_picked_siam_abs_lo_kernel(tc, xT, w1, w2, offs, out_0, out_1, out_2):
             plane = sb([P, T], F32, f"plane{j}")
             nc.sync.dma_start(plane[:], x_rows[:, j, :])
             planes.append(plane)
-        w1_raw = sb([P, PACK, H], F32, "w1_raw")
-        nc.sync.dma_start(w1_raw[:], w1.rearrange("(p j) c -> p j c", j=PACK))
-        w2_rows = w2.rearrange("(p j) c -> p j c", j=PACK)
-        w2_raw = []
-        for u in range(2):
-            half = sb([P, PACK, H // 2], F32, f"w2_raw{u}")
-            nc.sync.dma_start(half[:], w2_rows[:, :, u * 256 : (u + 1) * 256])
-            w2_raw.append(half)
+
+        def load_halves(w, name):
+            rows = w.rearrange("(p j) c -> p j c", j=PACK)
+            halves = []
+            for u in range(2):
+                half = sb([P, PACK, H // 2], F32, f"{name}{u}")
+                nc.sync.dma_start(half[:], rows[:, :, u * 256 : (u + 1) * 256])
+                halves.append(half)
+            return halves
+
+        w1_raw = load_halves(w1, "w1_raw")
+        w2_raw = load_halves(w2, "w2_raw")
 
         warm = sb([P, 8], F32, "warm")
         warm2 = sb([P, 8], F32, "warm2")
-        nc.gpsimd.memset(warm[:], 0.0)
+        nc.vector.memset(warm[:], 0.0)
         nc.scalar.activation(warm2[:], warm[:], ACT.Relu)
 
-        g01 = sb([P, 2, S], F32, "g01")
-        g23 = [sb([P, 2, V], F32, f"g23_{h}") for h in range(2)]
-        xg = [sb([P, V, PACK], BF16, f"xg{h}") for h in range(2)]
+        picked = sb([P, PACK, S], F32, "picked")
         xw = [sb([P, V], U32, f"xw{h}") for h in range(2)]
         xs = [sb([P, V], U8, f"xs{h}") for h in range(2)]
 
-        def weave_views(h, pair, src):
-            dst = xg[h][:, :, 2 * pair : 2 * pair + 2].rearrange("p (c i) t -> p c t i", i=4)
-            return dst, src.rearrange("p t (c i) -> p c t i", i=4)
+        def weave_views(dst_tile, dst_cols, src_cols, lo, hi):
+            dst = dst_tile[:, dst_cols, lo:hi].rearrange("p (c i) t -> p c t i", i=4)
+            src = picked[:, lo:hi, src_cols].rearrange("p t (c i) -> p c t i", i=4)
+            return dst, src
 
+        xgb = sb([P, V, PACK], BF16, "xgb")
         for j in range(2):
-            nc.vector.tensor_copy(g01[:, j, :], planes[j][:].indirect(offsets[:]))
+            nc.vector.tensor_copy(picked[:, j, :], planes[j][:].indirect(offsets[:]))
+        nc.scalar.copy(*weave_views(xgb, slice(0, V), slice(V, S), 0, 2))
+        nc.vector.tensor_copy(picked[:, 2, :], planes[2][:].indirect(offsets[:]))
         for h in (1, 0):
-            dst, src = weave_views(h, 0, g01[:, :, h * V : (h + 1) * V])
-            nc.scalar.activation(dst, src, ACT.Copy)
-        for j in range(2):
-            for h in (1, 0):
-                nc.vector.tensor_copy(g23[h][:, j, :], planes[2 + j][:].indirect(offsets[:, h * 16 : (h + 1) * 16]))
-        dst, src = weave_views(1, 1, g23[1][:])
-        nc.scalar.activation(dst, src, ACT.Copy)
-        dst, src = weave_views(0, 1, g23[0][:])
-        nc.vector.tensor_copy(dst, src)
-        for h in (1, 0):
-            quant(xw[h][:], xs[h][:], xg[h][:].rearrange("p c t -> p (c t)"))
+            nc.vector.tensor_copy(picked[:, 3, h * V : (h + 1) * V], planes[3][:].indirect(offsets[:, h * 16 : (h + 1) * 16]))
+        nc.vector.tensor_copy(*weave_views(xgb, slice(0, V), slice(V, S), 2, 4))
+        quant(xw[1][:], xs[1][:], xgb[:].rearrange("p c t -> p (c t)"))
 
-        w1_view = w1_raw[:].rearrange("p j (m t) -> p m j t", t=PACK)
+        def deal_views(grouped, raw, half, u):
+            dst = grouped[u][:, :, half * 64 : (half + 1) * 64, :].rearrange("p t m j -> p m j t")
+            return dst, raw[half][:].rearrange("p j (m t) -> p m j t", t=PACK)[:, :, :, 2 * u : 2 * u + 2]
+
+        def quant_w(words, scales, grouped, u):
+            quant(words[u][:], scales[u][:], grouped[u][:].rearrange("p t m j -> p (t m j)"))
+
         w1g = [sb([P, 2, P, PACK], BF16, f"w1g{u}") for u in range(2)]
-        w1w = sb([P, H], U32, "w1w")
-        w1s = sb([P, H], U8, "w1s")
-        nc.vector.tensor_copy(w1g[0][:].rearrange("p t m j -> p m j t"), w1_view[:, :, :, 0:2])
-        nc.scalar.activation(w1g[1][:].rearrange("p t m j -> p m j t"), w1_view[:, :, :, 2:4], ACT.Copy)
-        for t in range(PACK):
-            cols = slice(t * P, (t + 1) * P)
-            quant(w1w[:, cols], w1s[:, cols], w1g[t // 2][:, t % 2, :, :].rearrange("p m j -> p (m j)"))
+        w1w = [sb([P, 2 * P], U32, f"w1w{u}") for u in range(2)]
+        w1s = [sb([P, 2 * P], U8, f"w1s{u}") for u in range(2)]
+        nc.scalar.copy(*deal_views(w1g, w1_raw, 0, 0))
+        nc.scalar.copy(*deal_views(w1g, w1_raw, 0, 1))
+        nc.vector.tensor_copy(*deal_views(w1g, w1_raw, 1, 0))
+        nc.scalar.copy(*deal_views(w1g, w1_raw, 1, 1))
+        for u in range(2):
+            quant_w(w1w, w1s, w1g, u)
+        xga = sb([P, V, PACK], BF16, "xga", tag="w1_raw1")
+        for c in range(2):
+            cc = slice(c * CH, (c + 1) * CH)
+            nc.scalar.copy(*weave_views(xga, cc, cc, 0, 4))
+            quant(xw[0][:, cc], xs[0][:, cc], xga[:, cc, :].rearrange("p c t -> p (c t)"))
 
         hp = [[psum.tile([P, PACK, CH], F32, name=f"hp{h}{c}") for c in range(2)] for h in range(2)]
 
         def mm(out, lw, ls, t, rw, rs):
-            cols = slice(t * P, (t + 1) * P)
-            nc.tensor.matmul_mx(out=out, lhsT=lw[:, cols].bitcast(FP8X4), lhsT_scale=ls[:, cols],
+            cols = slice((t % 2) * P, (t % 2 + 1) * P)
+            nc.tensor.matmul_mx(out=out, lhsT=lw[t // 2][:, cols].bitcast(FP8X4), lhsT_scale=ls[t // 2][:, cols],
                                 rhs=rw.bitcast(FP8X4), rhs_scale=rs, start=True, stop=True)
 
-        def mm1(h, c, t):
-            cc = slice(c * CH, (c + 1) * CH)
-            mm(hp[h][c][:, t, :], w1w, w1s, t, xw[h][:, cc], xs[h][:, cc])
-
-        for t in range(PACK):
-            for h in (1, 0):
-                mm1(h, 0, t)
         for h in (1, 0):
-            for t in range(PACK):
-                mm1(h, 1, t)
+            for c in range(2):
+                cc = slice(c * CH, (c + 1) * CH)
+                for t in range(PACK):
+                    mm(hp[h][c][:, t, :], w1w, w1s, t, xw[h][:, cc], xs[h][:, cc])
 
-        w2g = [sb([P, PACK, P // 2, PACK], BF16, f"w2g{u}") for u in range(2)]
-        w2w = sb([P, H], U32, "w2w")
-        w2s = sb([P, H], U8, "w2s")
-
-        def w2_views(u):
-            return w2g[u][:].rearrange("p t m j -> p m j t"), w2_raw[u][:].rearrange("p j (m t) -> p m j t", t=PACK)
-
-        def w2_quant(u):
-            for t in range(PACK):
-                cols = slice(t * P + u * 64, t * P + (u + 1) * 64)
-                quant(w2w[:, cols], w2s[:, cols], w2g[u][:, t, :, :].rearrange("p m j -> p (m j)"))
+        w2g = [sb([P, 2, P, PACK], BF16, f"w2g{u}") for u in range(2)]
+        w2w = [sb([P, 2 * P], U32, f"w2w{u}") for u in range(2)]
+        w2s = [sb([P, 2 * P], U8, f"w2s{u}") for u in range(2)]
 
         rb = [sb([P, CH, PACK], F32, f"rb{c}") for c in range(2)]
         dz = [sb([P, CH, PACK], F32, f"dz{c}") for c in range(2)]
@@ -135,19 +132,19 @@ def tile_picked_siam_abs_lo_kernel(tc, xT, w1, w2, offs, out_0, out_1, out_2):
         def mag(c):
             nc.scalar.activation(zb[c][:], dz[c][:].rearrange("p v t -> p (v t)"), ACT.Abs)
 
-        dst, src = w2_views(0)
-        nc.vector.tensor_copy(dst, src)
         relu_b(0)
-        w2_quant(0)
-        diff(0)
         relu_b(1)
-        dst, src = w2_views(1)
-        nc.vector.tensor_copy(dst, src)
-        mag(0)
+        nc.scalar.copy(*deal_views(w2g, w2_raw, 0, 0))
+        nc.vector.tensor_copy(*deal_views(w2g, w2_raw, 0, 1))
+        diff(0)
         diff(1)
-        w2_quant(1)
-        quant(zw[0][:], zs[0][:], zb[0][:])
+        for u in range(2):
+            nc.vector.tensor_copy(*deal_views(w2g, w2_raw, 1, u))
+        mag(0)
         mag(1)
+        quant(zw[0][:], zs[0][:], zb[0][:])
+        for u in range(2):
+            quant_w(w2w, w2s, w2g, u)
         quant(zw[1][:], zs[1][:], zb[1][:])
 
         yp = [[psum.tile([P, 2, CH], F32, name=f"yp{c}{u}") for u in range(2)] for c in range(2)]

@@ -59,8 +59,14 @@ def tile_picked_siam_abs_lo_kernel(tc, xT, w1, w2, offs, out_0, out_1, out_2):
         nc.scalar.activation(warm2[:], warm[:], ACT.Relu)
 
         picked = sb([P, PACK, S], F32, "picked")
-        xw = [sb([P, V], U32, f"xw{h}") for h in range(2)]
-        xs = [sb([P, V], U8, f"xs{h}") for h in range(2)]
+        xw = {}
+        xs = {}
+
+        def quant_x(key, src, tag=None):
+            width = src.shape[1]
+            xw[key] = sb([P, width], U32, f"xw_{key}", tag=tag)
+            xs[key] = sb([P, width], U8, f"xs_{key}")
+            quant(xw[key][:], xs[key][:], src.rearrange("p c t -> p (c t)"))
 
         def weave_views(dst_tile, dst_cols, src_cols, lo, hi):
             dst = dst_tile[:, dst_cols, lo:hi].rearrange("p (c i) t -> p c t i", i=4)
@@ -75,7 +81,7 @@ def tile_picked_siam_abs_lo_kernel(tc, xT, w1, w2, offs, out_0, out_1, out_2):
         for h in (1, 0):
             nc.vector.tensor_copy(picked[:, 3, h * V : (h + 1) * V], planes[3][:].indirect(offsets[:, h * 16 : (h + 1) * 16]))
         nc.vector.tensor_copy(*weave_views(xgb, slice(0, V), slice(V, S), 2, 4))
-        quant(xw[1][:], xs[1][:], xgb[:].rearrange("p c t -> p (c t)"))
+        quant_x("b0", xgb[:, :CH, :])
 
         def deal_views(grouped, raw, half, u):
             dst = grouped[u][:, :, half * 64 : (half + 1) * 64, :].rearrange("p t m j -> p m j t")
@@ -93,11 +99,13 @@ def tile_picked_siam_abs_lo_kernel(tc, xT, w1, w2, offs, out_0, out_1, out_2):
         nc.scalar.copy(*deal_views(w1g, w1_raw, 1, 1))
         for u in range(2):
             quant_w(w1w, w1s, w1g, u)
+        quant_x("b1", xgb[:, CH:, :], tag="w1g1")
         xga = sb([P, V, PACK], BF16, "xga", tag="w1_raw1")
         for c in range(2):
             cc = slice(c * CH, (c + 1) * CH)
             nc.scalar.copy(*weave_views(xga, cc, cc, 0, 4))
-            quant(xw[0][:, cc], xs[0][:, cc], xga[:, cc, :].rearrange("p c t -> p (c t)"))
+            quant_x(f"a{c}", xga[:, cc, :])
+        moving = {(1, 0): ("b0", 0), (1, 1): ("b1", 0), (0, 0): ("a0", 0), (0, 1): ("a1", 0)}
 
         hp = [[psum.tile([P, PACK, CH], F32, name=f"hp{h}{c}") for c in range(2)] for h in range(2)]
 
@@ -106,14 +114,17 @@ def tile_picked_siam_abs_lo_kernel(tc, xT, w1, w2, offs, out_0, out_1, out_2):
             nc.tensor.matmul_mx(out=out, lhsT=lw[t // 2][:, cols].bitcast(FP8X4), lhsT_scale=ls[t // 2][:, cols],
                                 rhs=rw.bitcast(FP8X4), rhs_scale=rs, start=True, stop=True)
 
+        yp = [[psum.tile([P, 2, CH], F32, name=f"yp{c}{u}") for u in range(2)] for c in range(2)]
+        for r in range(6):
+            mm(yp[r % 2][r // 2 % 2][:, r // 4, :], [xw["b0"]], [xs["b0"]], 0, xw["b0"][:], xs["b0"][:])
         for h in (1, 0):
             for c in range(2):
-                cc = slice(c * CH, (c + 1) * CH)
+                key, first = moving[h, c]
+                cc = slice(first, first + CH)
                 for t in range(PACK):
-                    mm(hp[h][c][:, t, :], w1w, w1s, t, xw[h][:, cc], xs[h][:, cc])
+                    mm(hp[h][c][:, t, :], w1w, w1s, t, xw[key][:, cc], xs[key][:, cc])
 
         w2g = [sb([P, 2, P, PACK], BF16, f"w2g{u}") for u in range(2)]
-        w2w = [sb([P, 2 * P], U32, f"w2w{u}") for u in range(2)]
         w2s = [sb([P, 2 * P], U8, f"w2s{u}") for u in range(2)]
 
         rb = [sb([P, CH, PACK], F32, f"rb{c}") for c in range(2)]
@@ -140,6 +151,7 @@ def tile_picked_siam_abs_lo_kernel(tc, xT, w1, w2, offs, out_0, out_1, out_2):
         diff(1)
         for u in range(2):
             nc.vector.tensor_copy(*deal_views(w2g, w2_raw, 1, u))
+        w2w = [sb([P, 2 * P], U32, "w2w0"), sb([P, 2 * P], U32, "w2w1", tag="rb1")]
         mag(0)
         mag(1)
         quant(zw[0][:], zs[0][:], zb[0][:])
@@ -147,9 +159,8 @@ def tile_picked_siam_abs_lo_kernel(tc, xT, w1, w2, offs, out_0, out_1, out_2):
             quant_w(w2w, w2s, w2g, u)
         quant(zw[1][:], zs[1][:], zb[1][:])
 
-        yp = [[psum.tile([P, 2, CH], F32, name=f"yp{c}{u}") for u in range(2)] for c in range(2)]
         yf = [sb([P, PACK, CH], F32, f"yf{c}") for c in range(2)]
-        yb = [sb([P, CH, PACK], BF16, f"yb{c}") for c in range(2)]
+        yb = sb([P, V, PACK], BF16, "yb")
         yw = sb([P, V], U32, "yw")
         ys = sb([P, V], U8, "ys")
         y_rows = out_0.rearrange("(p t) v -> p t v", t=PACK)
@@ -162,10 +173,10 @@ def tile_picked_siam_abs_lo_kernel(tc, xT, w1, w2, offs, out_0, out_1, out_2):
             for u in range(2):
                 nc.scalar.copy(yf[c][:, 2 * u : 2 * u + 2, :], yp[c][u][:])
             nc.sync.dma_start(y_rows[:, :, cc], yf[c][:])
-            nc.vector.tensor_copy(yb[c][:].rearrange("p (c i) t -> p c t i", i=4),
+            nc.vector.tensor_copy(yb[:, cc, :].rearrange("p (c i) t -> p c t i", i=4),
                                   yf[c][:].rearrange("p t (c i) -> p c t i", i=4))
-            quant(yw[:, cc], ys[:, cc], yb[c][:].rearrange("p c t -> p (c t)"))
-            nc.sync.dma_start(y_words[:, cc], yw[:, cc].bitcast(I32))
+        quant(yw[:], ys[:], yb[:].rearrange("p c t -> p (c t)"))
+        nc.sync.dma_start(y_words, yw[:].bitcast(I32))
         for q in range(4):
             eng = nc.sync if q % 2 == 0 else nc.scalar
             eng.dma_start(y_scales[4 * q : 4 * q + 4, :], ys[32 * q : 32 * q + 4, :].bitcast(I32))

@@ -124,7 +124,7 @@ def tile_picked_siam_abs_lo_kernel(tc, xT, w1, w2, offs, out_0, out_1, out_2):
                 for t in range(PACK):
                     mm(hp[h][c][:, t, :], w1w, w1s, t, xw[key][:, cc], xs[key][:, cc])
 
-        w2g = [sb([P, 2, P, PACK], BF16, f"w2g{u}") for u in range(2)]
+        w2g = [sb([P, 2, P, PACK], BF16, "w2g0", tag="w1_raw1"), sb([P, 2, P, PACK], BF16, "w2g1")]
         w2s = [sb([P, 2 * P], U8, f"w2s{u}") for u in range(2)]
 
         rb = [sb([P, CH, PACK], F32, f"rb{c}") for c in range(2)]

from contextlib import ExitStack

import concourse.mybir as mybir

K, T, S, V, H = 512, 1024, 512, 256, 512
FLOPS = 2 * K * H * S + 2 * H * H * V

F32 = mybir.dt.float32
BF16 = mybir.dt.bfloat16
I32 = mybir.dt.int32
U32 = mybir.dt.uint32
U16 = mybir.dt.uint16
U8 = mybir.dt.uint8
FP8X4 = mybir.dt.float8_e4m3fn_x4
ACT = mybir.ActivationFunctionType
ALU = mybir.AluOpType

P = 128
PACK = 4
CH = 128


def tile_picked_siam_abs_lo_kernel(tc, xT, w1, w2, offs, out_0, out_1, out_2):
    nc = tc.nc
    with ExitStack() as ctx:
        keep = ctx.enter_context(tc.tile_pool(name="keep", bufs=1))
        psum = ctx.enter_context(tc.psum_pool(name="psum", bufs=1))

        def sb(shape, dtype, name, tag=None):
            return keep.tile(shape, dtype, name=name, tag=tag or name, align_bytes=64)

        def quant(words, scales, src):
            nc.vector.quantize_mx(out=words.bitcast(FP8X4), scales=scales, in_=src)

        offsets = keep.tile([P, S // 16], U16, name="offsets")
        nc.sync.dma_start(offsets[:], offs)
        x_rows = xT.rearrange("(p j) c -> p j c", j=PACK)
        planes = []
        for j in range(PACK):
            plane = sb([P, T], F32, f"plane{j}")
            nc.sync.dma_start(plane[:], x_rows[:, j, :])
            planes.append(plane)

        def load_halves(w, name):
            rows = w.rearrange("(p j) c -> p j c", j=PACK)
            halves = []
            for u in range(2):
                half = sb([P, PACK, H // 2], F32, f"{name}{u}")
                nc.sync.dma_start(half[:], rows[:, :, u * 256 : (u + 1) * 256])
                halves.append(half)
            return halves

        w1_raw = load_halves(w1, "w1_raw")
        w2_raw = load_halves(w2, "w2_raw")

        warm = sb([P, 8], F32, "warm")
        warm2 = sb([P, 8], F32, "warm2")
        nc.vector.memset(warm[:], 0.0)
        nc.scalar.activation(warm2[:], warm[:], ACT.Relu)

        picked = sb([P, PACK, S], F32, "picked")
        xw = {}
        xs = {}

        def quant_x(key, src, tag=None):
            width = src.shape[1]
            xw[key] = sb([P, width], U32, f"xw_{key}", tag=tag)
            xs[key] = sb([P, width], U8, f"xs_{key}")
            quant(xw[key][:], xs[key][:], src.rearrange("p c t -> p (c t)"))

        def weave_views(dst_tile, dst_cols, src_cols, lo, hi):
            dst = dst_tile[:, dst_cols, lo:hi].rearrange("p (c i) t -> p c t i", i=4)
            src = picked[:, lo:hi, src_cols].rearrange("p t (c i) -> p c t i", i=4)
            return dst, src

        xgb = sb([P, V, PACK], BF16, "xgb")
        for j in range(2):
            nc.vector.tensor_copy(picked[:, j, :], planes[j][:].indirect(offsets[:]))
        nc.scalar.copy(*weave_views(xgb, slice(0, V), slice(V, S), 0, 2))
        nc.vector.tensor_copy(picked[:, 2, :], planes[2][:].indirect(offsets[:]))
        for h in (1, 0):
            nc.vector.tensor_copy(picked[:, 3, h * V : (h + 1) * V], planes[3][:].indirect(offsets[:, h * 16 : (h + 1) * 16]))
        nc.vector.tensor_copy(*weave_views(xgb, slice(0, V), slice(V, S), 2, 4))
        quant_x("b0", xgb[:, :CH, :])

        def deal_views(grouped, raw, half, u):
            dst = grouped[u][:, :, half * 64 : (half + 1) * 64, :].rearrange("p t m j -> p m j t")
            return dst, raw[half][:].rearrange("p j (m t) -> p m j t", t=PACK)[:, :, :, 2 * u : 2 * u + 2]

        def quant_w(words, scales, grouped, u):
            quant(words[u][:], scales[u][:], grouped[u][:].rearrange("p t m j -> p (t m j)"))

        w1g = [sb([P, 2, P, PACK], BF16, f"w1g{u}") for u in range(2)]
        w1w = [sb([P, 2 * P], U32, f"w1w{u}") for u in range(2)]
        w1s = [sb([P, 2 * P], U8, f"w1s{u}") for u in range(2)]
        nc.scalar.copy(*deal_views(w1g, w1_raw, 0, 0))
        nc.scalar.copy(*deal_views(w1g, w1_raw, 0, 1))
        nc.vector.tensor_copy(*deal_views(w1g, w1_raw, 1, 0))
        nc.scalar.copy(*deal_views(w1g, w1_raw, 1, 1))
        for u in range(2):
            quant_w(w1w, w1s, w1g, u)
        quant_x("b1", xgb[:, CH:, :], tag="w1g1")
        xga = sb([P, V, PACK], BF16, "xga", tag="w1_raw1")
        for c in range(2):
            cc = slice(c * CH, (c + 1) * CH)
            nc.scalar.copy(*weave_views(xga, cc, cc, 0, 4))
            quant_x(f"a{c}", xga[:, cc, :])
        moving = {(1, 0): ("b0", 0), (1, 1): ("b1", 0), (0, 0): ("a0", 0), (0, 1): ("a1", 0)}

        hp = [[psum.tile([P, PACK, CH], F32, name=f"hp{h}{c}") for c in range(2)] for h in range(2)]

        def mm(out, lw, ls, t, rw, rs):
            cols = slice((t % 2) * P, (t % 2 + 1) * P)
            nc.tensor.matmul_mx(out=out, lhsT=lw[t // 2][:, cols].bitcast(FP8X4), lhsT_scale=ls[t // 2][:, cols],
                                rhs=rw.bitcast(FP8X4), rhs_scale=rs, start=True, stop=True)

        yp = [[psum.tile([P, 2, CH], F32, name=f"yp{c}{u}") for u in range(2)] for c in range(2)]
        for r in range(6):
            mm(yp[r % 2][r // 2 % 2][:, r // 4, :], [xw["b0"]], [xs["b0"]], 0, xw["b0"][:], xs["b0"][:])
        for h in (1, 0):
            for c in range(2):
                key, first = moving[h, c]
                cc = slice(first, first + CH)
                for t in range(PACK):
                    mm(hp[h][c][:, t, :], w1w, w1s, t, xw[key][:, cc], xs[key][:, cc])

        w2g = [sb([P, 2, P, PACK], BF16, "w2g0", tag="w1_raw1"), sb([P, 2, P, PACK], BF16, "w2g1")]
        w2s = [sb([P, 2 * P], U8, f"w2s{u}") for u in range(2)]

        rb = [sb([P, CH, PACK], F32, f"rb{c}") for c in range(2)]
        dz = [sb([P, CH, PACK], F32, f"dz{c}") for c in range(2)]
        zb = [sb([P, CH * PACK], BF16, f"zb{c}") for c in range(2)]
        zw = [sb([P, CH], U32, f"zw{c}") for c in range(2)]
        zs = [sb([P, CH], U8, f"zs{c}") for c in range(2)]

        def relu_b(c):
            nc.scalar.activation(rb[c][:], hp[1][c][:].rearrange("p t v -> p v t"), ACT.Relu)

        def diff(c):
            nc.vector.scalar_tensor_tensor(dz[c][:], hp[0][c][:].rearrange("p t v -> p v t"), 0.0, rb[c][:],
                                           ALU.max, ALU.subtract)

        def mag(c):
            nc.scalar.activation(zb[c][:], dz[c][:].rearrange("p v t -> p (v t)"), ACT.Abs)

        relu_b(0)
        relu_b(1)
        nc.scalar.copy(*deal_views(w2g, w2_raw, 0, 0))
        nc.vector.tensor_copy(*deal_views(w2g, w2_raw, 0, 1))
        diff(0)
        diff(1)
        for u in range(2):
            nc.vector.tensor_copy(*deal_views(w2g, w2_raw, 1, u))
        w2w = [sb([P, 2 * P], U32, "w2w0"), sb([P, 2 * P], U32, "w2w1", tag="rb1")]
        mag(0)
        mag(1)
        quant(zw[0][:], zs[0][:], zb[0][:])
        for u in range(2):
            quant_w(w2w, w2s, w2g, u)
        quant(zw[1][:], zs[1][:], zb[1][:])

        yf = [sb([P, PACK, CH], F32, f"yf{c}") for c in range(2)]
        yb = sb([P, V, PACK], BF16, "yb")
        yw = sb([P, V], U32, "yw")
        ys = sb([P, V], U8, "ys")
        y_rows = out_0.rearrange("(p t) v -> p t v", t=PACK)
        y_words = out_1[0].rearrange("p c r -> p (c r)").bitcast(I32)
        y_scales = out_2[0].bitcast(I32)
        for c in range(2):
            cc = slice(c * CH, (c + 1) * CH)
            for t in range(PACK):
                mm(yp[c][t // 2][:, t % 2, :], w2w, w2s, t, zw[c][:], zs[c][:])
            for u in range(2):
                nc.scalar.copy(yf[c][:, 2 * u : 2 * u + 2, :], yp[c][u][:])
            nc.sync.dma_start(y_rows[:, :, cc], yf[c][:])
            nc.vector.tensor_copy(yb[:, cc, :].rearrange("p (c i) t -> p c t i", i=4),
                                  yf[c][:].rearrange("p t (c i) -> p c t i", i=4))
        quant(yw[:], ys[:], yb[:].rearrange("p c t -> p (c t)"))
        nc.sync.dma_start(y_words, yw[:].bitcast(I32))
        for q in range(4):
            eng = nc.sync if q % 2 == 0 else nc.scalar
            eng.dma_start(y_scales[4 * q : 4 * q + 4, :], ys[32 * q : 32 * q + 4, :].bitcast(I32))
